import numpy as np
import ml_dtypes


def mxq(x, axis, fmt="e4m3"):
    dtype, down = {"e4m3": (ml_dtypes.float8_e4m3fn, 7), "e5m2": (ml_dtypes.float8_e5m2, 14)}[fmt]
    v = np.moveaxis(np.asarray(x, np.float32).astype(ml_dtypes.bfloat16).astype(np.float64), axis, -1)
    blocks = v.reshape(v.shape[:-1] + (-1, 32))
    amax = np.abs(blocks).max(-1, keepdims=True)
    byte = np.maximum(np.where(amax > 0, np.frexp(amax)[1] - 1 + 127, 0) - down, 1)
    scale = np.exp2(byte - 127.0)
    codes = (blocks / scale).astype(np.float32).astype(dtype).astype(np.float64)
    return np.moveaxis((codes * scale).reshape(v.shape), -1, axis)


WIDE = False


def mx_kscale(k):
    if not WIDE:
        return np.ones(k)
    levels = np.array([30, -30])
    if k % 512:
        return np.exp2(np.random.permutation(np.resize(levels, k // 32))).repeat(32)
    a = np.empty((k // 512, 16))
    for p in range(k // 512):
        a[p, :8] = np.random.permutation(np.resize(levels, 8))
        for g in range(8):
            far = levels[np.abs(levels - a[p, g]) >= 10]
            a[p, g + 8] = far[np.random.randint(len(far))]
    return np.exp2(a.ravel()).repeat(32)


BF16 = ml_dtypes.bfloat16


def bf(x):
    return np.asarray(x, np.float32).astype(BF16)


def f64(x):
    return np.asarray(x).astype(np.float64)


M, R, KX, KG, KY = 1024, 1024, 1024, 512, 1536
TAIL = 0.75
BIAS = 0.5


def setup_inputs():
    a, b, d = mx_kscale(KX), mx_kscale(KG), mx_kscale(KY)
    normal = np.random.standard_normal
    tail = np.exp(TAIL * normal((M, KG)) - TAIL * TAIL)
    return {"x": bf(normal((M, KX)) * a),
            "g": bf(normal((M, KG)) * tail * b),
            "y": bf(normal((M, KY)) * d),
            "sx": bf(normal((KX, R)) / np.sqrt(KX) / a[:, None]),
            "sg": bf(normal((KG, R)) / np.sqrt(KG) / b[:, None]),
            "sy": bf(normal((KY, R)) / np.sqrt(KY) / d[:, None]),
            "c": bf(BIAS * normal(R)),
            "r": bf(1 + 0.1 * normal(M))}


def reference(x, g, y, sx, sg, sy, c, r):
    px = mxq(f64(x), 1, "e4m3") @ mxq(f64(sx), 0, "e4m3")
    pg = mxq(f64(g), 1, "e5m2") @ mxq(f64(sg), 0, "e4m3")
    u = px + pg
    v = (mxq(f64(y), 1, "e4m3") @ mxq(f64(sy), 0, "e4m3")) + f64(c)
    return u * v * f64(r)[:, None]

@@ -1,0 +1,278 @@
+from contextlib import ExitStack
+
+import concourse.mybir as mybir
+from concourse.masks import make_identity
+
+M, R = 1024, 1024
+K_TOTAL = 1024 + 512 + 1536
+FLOPS = 2 * M * R * K_TOTAL
+
+F32 = mybir.dt.float32
+BF16 = mybir.dt.bfloat16
+U32 = mybir.dt.uint32
+U8 = mybir.dt.uint8
+E4M3X4 = mybir.dt.float8_e4m3fn_x4
+E5M2X4 = mybir.dt.float8_e5m2_x4
+ALU = mybir.AluOpType
+
+P = 128
+PACK = 4
+SPAN = P * PACK
+PASSES = 3
+CHUNKS = 12
+TILES = 4
+QUARTERS = 8
+PSUM_BUFS = 4
+STAGE_BUFS = 4
+RAW_BUFS = 8
+OUT_BUFS = 4
+SHARED_WEIGHT_CHUNKS = 9
+
+LOAD_ORDER = "W0 A0 A1 W1 A2 A3 W2 A4 A5 W3 W4 W5 A6 A7 W6 W7 A8 A9 W8 W9 A10 A11 W10 W11"
+SCALAR_HALVES_BEFORE_PAIR = (1, 1, 1, 4, 3, 3)
+VECTOR_ORDER = (
+    "I0 W0 A0 I1 A1 W1 I2 A2 A3 W2 I3 A4 E A5 E E E W3 E I4 I5 W4 W5 E E E E E E I6 E W6 A6 I7 A7 "
+    "E W7 I8 A8 W8 E E E A9 A10 E A11 E E E W9 E W10 W11 E E E E E E E E E E E"
+)
+
+
+def chunk_of(factor, half, k_pass):
+    return (factor * 2 + half) * PASSES + k_pass
+
+
+def quarter_parts(quarter):
+    return quarter // 4, quarter % 2, (quarter // 2) % 2
+
+
+def tensor_order():
+    by_pass = [[("mm", 0, j, k_pass) for j in range(TILES)] for k_pass in range(PASSES)]
+    by_tile = [
+        [("mm", q, j, k_pass) for j in range(TILES) for k_pass in range(PASSES)] for q in range(QUARTERS)
+    ]
+    after_pair = [by_pass[0], by_pass[1], by_pass[2] + by_tile[1], by_tile[2], by_tile[3], sum(by_tile[4:], [])]
+    order = [("turn_c",)]
+    for pair in range(CHUNKS // 2):
+        order += [("turn", c, b) for c in (2 * pair, 2 * pair + 1) for b in range(2)]
+        order += after_pair[pair]
+    return order
+
+
+def scalar_order():
+    halves = [("weave", c, 0) for c in range(SHARED_WEIGHT_CHUNKS)]
+    halves += [("weave", c, h) for c in range(SHARED_WEIGHT_CHUNKS, CHUNKS) for h in range(2)]
+    order, used = [], 0
+    for pair, count in enumerate(SCALAR_HALVES_BEFORE_PAIR):
+        order += halves[used : used + count]
+        used += count
+        if pair == 0:
+            order.append(("empty_c",))
+        order += [("empty", c, b) for c in (2 * pair, 2 * pair + 1) for b in range(2)]
+    return order + halves[used:]
+
+
+def vector_order():
+    order, finished = [], 0
+    for token in VECTOR_ORDER.split():
+        if token == "E":
+            order.append(("finish", finished // TILES, finished % TILES))
+            finished += 1
+        elif token.startswith("I"):
+            order.append(("weave", int(token[1:]), 1))
+        else:
+            order.append(("quantise", token[0], int(token[1:])))
+    return order
+
+
+def sync_order():
+    loads = [("load", token[0], int(token[1:])) for token in LOAD_ORDER.split()]
+    return loads + [("store", q, j) for q in range(QUARTERS // 2, QUARTERS) for j in range(TILES)]
+
+
+def producers(step):
+    kind = step[0]
+    if kind == "turn":
+        return [("load", "A", step[1])]
+    if kind == "empty":
+        return [("turn", step[1], step[2])]
+    if kind == "empty_c":
+        return [("turn_c",)]
+    if kind == "weave":
+        return [("load", "W", step[1])]
+    if kind == "quantise":
+        made_by = "empty" if step[1] == "A" else "weave"
+        return [(made_by, step[2], 0), (made_by, step[2], 1)]
+    if kind == "mm":
+        factor, m_half, n_half = quarter_parts(step[1])
+        return [
+            ("quantise", "A", chunk_of(factor, m_half, step[3])),
+            ("quantise", "W", chunk_of(factor, n_half, step[3])),
+        ]
+    if kind == "finish":
+        return [("mm", step[1], step[2], PASSES - 1), ("empty_c",)]
+    if kind == "store":
+        return [("finish", step[1], step[2])]
+    return []
+
+
+def merged(orders):
+    written, text = set(), []
+    position = [0] * len(orders)
+    while len(text) < sum(len(order) for order in orders):
+        before = len(text)
+        for e, order in enumerate(orders):
+            if position[e] < len(order) and all(p in written for p in producers(order[position[e]])):
+                written.add(order[position[e]])
+                text.append(order[position[e]])
+                position[e] += 1
+        assert len(text) > before
+    return text
+
+
+def tile_kronecker_gradient_sketch_s2_kernel(tc, x, g, y, sx, sg, sy, c, r, out):
+    nc = tc.nc
+    sources = [
+        [(y, sy, 0, E4M3X4), (y, sy, SPAN, E4M3X4), (y, sy, 2 * SPAN, E4M3X4)],
+        [(x, sx, 0, E4M3X4), (x, sx, SPAN, E4M3X4), (g, sg, 0, E5M2X4)],
+    ]
+
+    with ExitStack() as ctx:
+        keep = ctx.enter_context(tc.tile_pool(name="keep", bufs=1))
+        raw_pool = ctx.enter_context(tc.tile_pool(name="raw", bufs=RAW_BUFS))
+        stage_pool = ctx.enter_context(tc.tile_pool(name="stage", bufs=STAGE_BUFS))
+        out_pool = ctx.enter_context(tc.tile_pool(name="result", bufs=OUT_BUFS))
+        turn_psum = ctx.enter_context(tc.psum_pool(name="turn", bufs=PSUM_BUFS))
+        sum_psum = ctx.enter_context(tc.psum_pool(name="sums", bufs=PSUM_BUFS))
+        ctx.enter_context(tc.manual_schedule())
+
+        ident = keep.tile([P, P], F32)
+        make_identity(nc, ident[:])
+        c_rows = keep.tile([P, R // P], BF16)
+        nc.scalar.dma_start(out=c_rows[:], in_=c.rearrange("(p j) -> p j", p=P))
+        r_rows = keep.tile([P, 2, TILES], BF16)
+        nc.scalar.dma_start(out=r_rows[:], in_=r.rearrange("(h p j) -> p h j", h=2, p=P))
+        c_all = keep.tile([P, R], BF16)
+
+        raw, staged, codes, scales, banks, sums, second, results = {}, {}, {}, {}, {}, {}, {}, {}
+
+        def source(chunk):
+            return sources[chunk // (2 * PASSES)][chunk % PASSES], (chunk // PASSES) % 2
+
+        def stage_tile(side, chunk):
+            if (side, chunk) not in staged:
+                staged[side, chunk] = stage_pool.tile(
+                    [P, SPAN * PACK], BF16, name="staged_" + side, align_bytes=256
+                )
+            return staged[side, chunk]
+
+        def load(side, chunk):
+            (samples, weights, k0, fmt), half = source(chunk)
+            span = slice(half * SPAN, (half + 1) * SPAN)
+            k_span = slice(k0, k0 + SPAN)
+            rows = samples[span, k_span] if side == "A" else weights[k_span, span]
+            raw[side, chunk] = raw_pool.tile([P, PACK, SPAN], BF16, name="raw_" + side, align_bytes=256)
+            nc.sync.dma_start(out=raw[side, chunk][:], in_=rows.rearrange("(p j) w -> p j w", j=PACK))
+
+        def turn_c():
+            words = c_rows[:].bitcast(F32)
+            banks["c"] = turn_psum.tile([P, 4, P], F32, name="bank")
+            for j in range(4):
+                nc.tensor.transpose(banks["c"][:, j, :], words[:, j : j + 1].to_broadcast([P, P]), ident[:])
+
+        def empty_c():
+            nc.scalar.copy(
+                out=c_all[:].bitcast(F32).rearrange("p (n j) -> p n j", j=4),
+                in_=banks["c"][:].rearrange("p j n -> p n j"),
+            )
+
+        def turn(chunk, b):
+            words = raw["A", chunk][:].rearrange("p j k -> p (j k)").bitcast(F32)
+            banks[chunk, b] = turn_psum.tile([P, 2, 2 * P], F32, name="bank")
+            for t in range(2):
+                first = (2 * b + t) * 2 * P
+                for u in range(2):
+                    nc.tensor.transpose(
+                        banks[chunk, b][:, u, t * P : (t + 1) * P],
+                        words[:, first + u : first + 2 * P : 2],
+                        ident[:],
+                    )
+
+        def empty(chunk, b):
+            words = stage_tile("A", chunk)[:].bitcast(F32)
+            nc.scalar.copy(
+                out=words[:, b * SPAN : (b + 1) * SPAN].rearrange("p (m u) -> p m u", u=2),
+                in_=banks[chunk, b][:].rearrange("p u m -> p m u"),
+            )
+
+        def weave(chunk, h):
+            width = SPAN // 2
+            dst = stage_tile("W", chunk)[:, h * width * PACK : (h + 1) * width * PACK]
+            src = raw["W", chunk][:, :, h * width : (h + 1) * width]
+            dst = dst.rearrange("p (n i t) -> p n t i", i=4, t=PACK)
+            src = src.rearrange("p t (n i) -> p n t i", i=4)
+            if h == 1 and chunk < SHARED_WEIGHT_CHUNKS:
+                nc.vector.tensor_copy(out=dst, in_=src)
+            else:
+                nc.scalar.copy(out=dst, in_=src)
+
+        def code_format(side, chunk):
+            return source(chunk)[0][3] if side == "A" else E4M3X4
+
+        def quantise(side, chunk):
+            codes[side, chunk] = keep.tile([P, SPAN], U32, name="codes_%s%d" % (side, chunk), align_bytes=256)
+            scales[side, chunk] = keep.tile([P, SPAN], U8, name="scales_%s%d" % (side, chunk), align_bytes=256)
+            nc.vector.quantize_mx(
+                out=codes[side, chunk][:].bitcast(code_format(side, chunk)),
+                scales=scales[side, chunk][:],
+                in_=staged[side, chunk][:],
+            )
+
+        def mm(quarter, j, k_pass):
+            factor, m_half, n_half = quarter_parts(quarter)
+            a, w = chunk_of(factor, m_half, k_pass), chunk_of(factor, n_half, k_pass)
+            if k_pass == 0:
+                sums[quarter, j] = sum_psum.tile([P, SPAN], F32, name="acc")
+            cols = slice(j * P, (j + 1) * P)
+            nc.tensor.matmul_mx(
+                out=sums[quarter, j][:],
+                lhsT=codes["A", a][:, cols].bitcast(code_format("A", a)),
+                lhsT_scale=scales["A", a][:, cols],
+                rhs=codes["W", w][:].bitcast(E4M3X4),
+                rhs_scale=scales["W", w][:],
+                start=(k_pass == 0),
+                stop=(k_pass == PASSES - 1),
+            )
+
+        def finish(quarter, j):
+            factor, m_half, n_half = quarter_parts(quarter)
+            if factor == 0:
+                second[quarter, j] = keep.tile([P, SPAN], F32, name="second_%d_%d" % (quarter, j))
+                nc.vector.tensor_tensor(
+                    out=second[quarter, j][:],
+                    in0=sums[quarter, j][:],
+                    in1=c_all[:, n_half * SPAN : (n_half + 1) * SPAN],
+                    op=ALU.add,
+                )
+            else:
+                results[quarter, j] = out_pool.tile([P, SPAN], F32, name="result")
+                nc.vector.scalar_tensor_tensor(
+                    out=results[quarter, j][:],
+                    in0=sums[quarter, j][:],
+                    scalar=r_rows[:, m_half, j : j + 1],
+                    in1=second[quarter - QUARTERS // 2, j][:],
+                    op0=ALU.mult,
+                    op1=ALU.mult,
+                )
+
+        def store(quarter, j):
+            factor, m_half, n_half = quarter_parts(quarter)
+            block = out[m_half * SPAN : (m_half + 1) * SPAN, n_half * SPAN : (n_half + 1) * SPAN]
+            nc.sync.dma_start(
+                out=block.rearrange("(p j) n -> p j n", j=TILES)[:, j, :], in_=results[quarter, j][:]
+            )
+
+        emit = {
+            "load": load, "turn_c": turn_c, "empty_c": empty_c, "turn": turn, "empty": empty, "weave": weave,
+            "quantise": quantise, "mm": mm, "finish": finish, "store": store,
+        }
+        for step in merged([sync_order(), tensor_order(), scalar_order(), vector_order()]):
+            emit[step[0]](*step[1:])

@@ -25,15 +25,21 @@ QUARTERS = 8
 PSUM_BUFS = 4
 STAGE_BUFS = 4
 RAW_BUFS = 8
-OUT_BUFS = 4
-SHARED_WEIGHT_CHUNKS = 9
+OUT_BUFS = 6
+LATE_BY_PASS_QUARTER = 6
 
-LOAD_ORDER = "W0 A0 A1 W1 A2 A3 W2 A4 A5 W3 W4 W5 A6 A7 W6 W7 A8 A9 W8 W9 A10 A11 W10 W11"
-SCALAR_HALVES_BEFORE_PAIR = (1, 1, 1, 4, 3, 3)
+LOAD_ORDER = "W0 A0a A0b A1a A1b W1 A2 A3 W2 A4 A5 W3 W4 W5 A6 A7 W6 W7 A8 A9 W8 W9 A10 A11 W10 W11"
+SCALAR_HALVES_BEFORE_PAIR = (1, 0, 0, 4, 3, 3)
 VECTOR_ORDER = (
-    "I0 W0 A0 I1 A1 W1 I2 A2 A3 W2 I3 A4 E A5 E E E W3 E I4 I5 W4 W5 E E E E E E I6 E W6 A6 I7 A7 "
-    "E W7 I8 A8 W8 E E E A9 A10 E A11 E E E W9 E W10 W11 E E E E E E E E E E E"
+    "I0b C W0 A0a A0b A1a I1a I1b A1b W1 I2a I2b A2 W2 A3 A4a I3b A4b E A5a E E A5b E W3 E I4b E W4 W5 "
+    "E E E E I6b E E W6 A6 W7 A7 E A8 E E A9 E W8 I10b A10 E A11 E E E W9 E E W10 E W11 E E E E E E E E E"
 )
+
+
+def parse(token):
+    if token[-1] in "ab":
+        return token[0], int(token[1:-1]), ("ab".index(token[-1]),)
+    return token[0], int(token[1:]), (0, 1)
 
 
 def chunk_of(factor, half, k_pass):
@@ -45,85 +51,120 @@ def quarter_parts(quarter):
 
 
 def tensor_order():
-    by_pass = [[("mm", 0, j, k_pass) for j in range(TILES)] for k_pass in range(PASSES)]
-    by_tile = [
-        [("mm", q, j, k_pass) for j in range(TILES) for k_pass in range(PASSES)] for q in range(QUARTERS)
+    def by_pass(quarter, k_pass):
+        return [("mm", quarter, j, k_pass) for j in range(TILES)]
+
+    def whole(quarter):
+        if quarter == LATE_BY_PASS_QUARTER:
+            return [step for k_pass in range(PASSES) for step in by_pass(quarter, k_pass)]
+        return [("mm", quarter, j, k_pass) for j in range(TILES) for k_pass in range(PASSES)]
+
+    after_pair = [
+        by_pass(0, 0),
+        by_pass(0, 1),
+        by_pass(0, 2) + whole(1),
+        whole(2),
+        whole(3),
+        whole(4) + whole(5) + whole(6) + whole(7),
     ]
-    after_pair = [by_pass[0], by_pass[1], by_pass[2] + by_tile[1], by_tile[2], by_tile[3], sum(by_tile[4:], [])]
     order = [("turn_c",)]
     for pair in range(CHUNKS // 2):
-        order += [("turn", c, b) for c in (2 * pair, 2 * pair + 1) for b in range(2)]
+        order += [("turn", chunk, h) for chunk in (2 * pair, 2 * pair + 1) for h in range(2)]
         order += after_pair[pair]
     return order
 
 
-def scalar_order():
-    halves = [("weave", c, 0) for c in range(SHARED_WEIGHT_CHUNKS)]
-    halves += [("weave", c, h) for c in range(SHARED_WEIGHT_CHUNKS, CHUNKS) for h in range(2)]
-    order, used = [], 0
-    for pair, count in enumerate(SCALAR_HALVES_BEFORE_PAIR):
-        order += halves[used : used + count]
-        used += count
-        if pair == 0:
-            order.append(("empty_c",))
-        order += [("empty", c, b) for c in (2 * pair, 2 * pair + 1) for b in range(2)]
-    return order + halves[used:]
+def column_parts(quarter, j):
+    last = quarter == QUARTERS - 1 and j == TILES - 1
+    return [(0, SPAN // 2), (SPAN // 2, SPAN)] if last else [(0, SPAN)]
 
 
 def vector_order():
     order, finished = [], 0
     for token in VECTOR_ORDER.split():
         if token == "E":
-            order.append(("finish", finished // TILES, finished % TILES))
+            quarter, j = divmod(finished, TILES)
+            order += [("finish", quarter, j, part) for part in column_parts(quarter, j)]
             finished += 1
+        elif token == "C":
+            order.append(("empty_c",))
         elif token.startswith("I"):
-            order.append(("weave", int(token[1:]), 1))
+            order.append(("weave", parse(token)[1], parse(token)[2][0], "vector"))
         else:
-            order.append(("quantise", token[0], int(token[1:])))
+            order.append(("quantise",) + parse(token))
     return order
 
 
+def scalar_order():
+    on_vector = [step[1:3] for step in vector_order() if step[0] == "weave"]
+    halves = [
+        ("weave", chunk, h, "scalar") for chunk in range(CHUNKS) for h in range(2) if (chunk, h) not in on_vector
+    ]
+    order, used = [], 0
+    for pair, count in enumerate(SCALAR_HALVES_BEFORE_PAIR):
+        order += halves[used : used + count]
+        used += count
+        order += [("empty", chunk, h) for chunk in (2 * pair, 2 * pair + 1) for h in range(2)]
+    return order + halves[used:]
+
+
 def sync_order():
-    loads = [("load", token[0], int(token[1:])) for token in LOAD_ORDER.split()]
-    return loads + [("store", q, j) for q in range(QUARTERS // 2, QUARTERS) for j in range(TILES)]
+    loads = [("load",) + parse(token) for token in LOAD_ORDER.split()]
+    stores = [
+        ("store", quarter, j, part)
+        for quarter in range(QUARTERS // 2, QUARTERS)
+        for j in range(TILES)
+        for part in column_parts(quarter, j)
+    ]
+    return loads + stores
 
 
-def producers(step):
+def makes(step):
+    if step[0] in ("load", "quantise"):
+        return [step[:3] + (h,) for h in step[3]]
+    if step[0] == "weave":
+        return [step[:3]]
+    return [step]
+
+
+def needs(step):
     kind = step[0]
     if kind == "turn":
-        return [("load", "A", step[1])]
+        return [("load", "A") + step[1:]]
     if kind == "empty":
-        return [("turn", step[1], step[2])]
+        return [("turn",) + step[1:]]
     if kind == "empty_c":
         return [("turn_c",)]
     if kind == "weave":
-        return [("load", "W", step[1])]
+        return [("load", "W") + step[1:3]]
     if kind == "quantise":
-        made_by = "empty" if step[1] == "A" else "weave"
-        return [(made_by, step[2], 0), (made_by, step[2], 1)]
+        return [("empty" if step[1] == "A" else "weave", step[2], h) for h in step[3]]
     if kind == "mm":
         factor, m_half, n_half = quarter_parts(step[1])
+        weights = chunk_of(factor, n_half, step[3])
         return [
-            ("quantise", "A", chunk_of(factor, m_half, step[3])),
-            ("quantise", "W", chunk_of(factor, n_half, step[3])),
+            ("quantise", "A", chunk_of(factor, m_half, step[3]), step[2] // 2),
+            ("quantise", "W", weights, 0),
+            ("quantise", "W", weights, 1),
         ]
     if kind == "finish":
-        return [("mm", step[1], step[2], PASSES - 1), ("empty_c",)]
+        return [("mm", step[1], step[2], PASSES - 1)]
     if kind == "store":
-        return [("finish", step[1], step[2])]
+        return [("finish",) + step[1:]]
     return []
 
 
 def merged(orders):
-    written, text = set(), []
+    made, text = set(), []
     position = [0] * len(orders)
     while len(text) < sum(len(order) for order in orders):
         before = len(text)
         for e, order in enumerate(orders):
-            if position[e] < len(order) and all(p in written for p in producers(order[position[e]])):
-                written.add(order[position[e]])
+            if position[e] < len(order) and all(key in made for key in needs(order[position[e]])):
                 text.append(order[position[e]])
                 position[e] += 1
+                for key in makes(text[-1]):
+                    made.add(key)
         assert len(text) > before
     return text
 
@@ -164,13 +205,17 @@ def tile_kronecker_gradient_sketch_s2_kernel(tc, x, g, y, sx, sg, sy, c, r, out)
                 )
             return staged[side, chunk]
 
-        def load(side, chunk):
+        def load(side, chunk, halves):
             (samples, weights, k0, fmt), half = source(chunk)
             span = slice(half * SPAN, (half + 1) * SPAN)
             k_span = slice(k0, k0 + SPAN)
             rows = samples[span, k_span] if side == "A" else weights[k_span, span]
-            raw[side, chunk] = raw_pool.tile([P, PACK, SPAN], BF16, name="raw_" + side, align_bytes=256)
-            nc.sync.dma_start(out=raw[side, chunk][:], in_=rows.rearrange("(p j) w -> p j w", j=PACK))
+            if halves[0] == 0:
+                raw[side, chunk] = raw_pool.tile([P, PACK, SPAN], BF16, name="raw_" + side, align_bytes=256)
+            js = slice(2 * halves[0], 2 * halves[-1] + 2)
+            nc.sync.dma_start(
+                out=raw[side, chunk][:, js, :], in_=rows.rearrange("(p j) w -> p j w", j=PACK)[:, js, :]
+            )
 
         def turn_c():
             words = c_rows[:].bitcast(F32)
@@ -179,7 +224,7 @@ def tile_kronecker_gradient_sketch_s2_kernel(tc, x, g, y, sx, sg, sy, c, r, out)
                 nc.tensor.transpose(banks["c"][:, j, :], words[:, j : j + 1].to_broadcast([P, P]), ident[:])
 
         def empty_c():
-            nc.scalar.copy(
+            nc.vector.tensor_copy(
                 out=c_all[:].bitcast(F32).rearrange("p (n j) -> p n j", j=4),
                 in_=banks["c"][:].rearrange("p j n -> p n j"),
             )
@@ -203,13 +248,13 @@ def tile_kronecker_gradient_sketch_s2_kernel(tc, x, g, y, sx, sg, sy, c, r, out)
                 in_=banks[chunk, b][:].rearrange("p u m -> p m u"),
             )
 
-        def weave(chunk, h):
+        def weave(chunk, h, engine):
             width = SPAN // 2
             dst = stage_tile("W", chunk)[:, h * width * PACK : (h + 1) * width * PACK]
             src = raw["W", chunk][:, :, h * width : (h + 1) * width]
             dst = dst.rearrange("p (n i t) -> p n t i", i=4, t=PACK)
             src = src.rearrange("p t (n i) -> p n t i", i=4)
-            if h == 1 and chunk < SHARED_WEIGHT_CHUNKS:
+            if engine == "vector":
                 nc.vector.tensor_copy(out=dst, in_=src)
             else:
                 nc.scalar.copy(out=dst, in_=src)
@@ -217,20 +262,24 @@ def tile_kronecker_gradient_sketch_s2_kernel(tc, x, g, y, sx, sg, sy, c, r, out)
         def code_format(side, chunk):
             return source(chunk)[0][3] if side == "A" else E4M3X4
 
-        def quantise(side, chunk):
-            codes[side, chunk] = keep.tile([P, SPAN], U32, name="codes_%s%d" % (side, chunk), align_bytes=256)
-            scales[side, chunk] = keep.tile([P, SPAN], U8, name="scales_%s%d" % (side, chunk), align_bytes=256)
+        def quantise(side, chunk, halves):
+            if halves[0] == 0:
+                label = "%s%d" % (side, chunk)
+                codes[side, chunk] = keep.tile([P, SPAN], U32, name="codes_" + label, align_bytes=256)
+                scales[side, chunk] = keep.tile([P, SPAN], U8, name="scales_" + label, align_bytes=256)
+            first, end = halves[0] * SPAN // 2, (halves[-1] + 1) * SPAN // 2
             nc.vector.quantize_mx(
-                out=codes[side, chunk][:].bitcast(code_format(side, chunk)),
-                scales=scales[side, chunk][:],
-                in_=staged[side, chunk][:],
+                out=codes[side, chunk][:, first:end].bitcast(code_format(side, chunk)),
+                scales=scales[side, chunk][:, first:end],
+                in_=staged[side, chunk][:, first * PACK : end * PACK],
             )
 
         def mm(quarter, j, k_pass):
             factor, m_half, n_half = quarter_parts(quarter)
             a, w = chunk_of(factor, m_half, k_pass), chunk_of(factor, n_half, k_pass)
             if k_pass == 0:
-                sums[quarter, j] = sum_psum.tile([P, SPAN], F32, name="acc")
+                pool = turn_psum if quarter == LATE_BY_PASS_QUARTER else sum_psum
+                sums[quarter, j] = pool.tile([P, SPAN], F32, name="bank")
             cols = slice(j * P, (j + 1) * P)
             nc.tensor.matmul_mx(
                 out=sums[quarter, j][:],
@@ -242,7 +291,7 @@ def tile_kronecker_gradient_sketch_s2_kernel(tc, x, g, y, sx, sg, sy, c, r, out)
                 stop=(k_pass == PASSES - 1),
             )
 
-        def finish(quarter, j):
+        def finish(quarter, j, part):
             factor, m_half, n_half = quarter_parts(quarter)
             if factor == 0:
                 second[quarter, j] = keep.tile([P, SPAN], F32, name="second_%d_%d" % (quarter, j))
@@ -253,21 +302,22 @@ def tile_kronecker_gradient_sketch_s2_kernel(tc, x, g, y, sx, sg, sy, c, r, out)
                     op=ALU.add,
                 )
             else:
-                results[quarter, j] = out_pool.tile([P, SPAN], F32, name="result")
+                cols = slice(*part)
+                results[quarter, j, part] = out_pool.tile([P, part[1] - part[0]], F32, name="result")
                 nc.vector.scalar_tensor_tensor(
-                    out=results[quarter, j][:],
-                    in0=sums[quarter, j][:],
+                    out=results[quarter, j, part][:],
+                    in0=sums[quarter, j][:, cols],
                     scalar=r_rows[:, m_half, j : j + 1],
-                    in1=second[quarter - QUARTERS // 2, j][:],
+                    in1=second[quarter - QUARTERS // 2, j][:, cols],
                     op0=ALU.mult,
                     op1=ALU.mult,
                 )
 
-        def store(quarter, j):
+        def store(quarter, j, part):
             factor, m_half, n_half = quarter_parts(quarter)
-            block = out[m_half * SPAN : (m_half + 1) * SPAN, n_half * SPAN : (n_half + 1) * SPAN]
+            block = out[m_half * SPAN : (m_half + 1) * SPAN, n_half * SPAN + part[0] : n_half * SPAN + part[1]]
             nc.sync.dma_start(
-                out=block.rearrange("(p j) n -> p j n", j=TILES)[:, j, :], in_=results[quarter, j][:]
+                out=block.rearrange("(p j) n -> p j n", j=TILES)[:, j, :], in_=results[quarter, j, part][:]
             )
 
         emit = {

@@ -29,11 +29,16 @@ OUT_BUFS = 6
 LATE_BY_PASS_QUARTER = 6
 
 LOAD_ORDER = "W0 A0a A0b A1a A1b W1 A2 A3 W2 A4 A5 W3 W4 W5 A6 A7 W6 W7 A8 A9 W8 W9 A10 A11 W10 W11"
-SCALAR_HALVES_BEFORE_PAIR = (1, 0, 0, 4, 3, 3)
-VECTOR_ORDER = (
-    "I0b C W0 A0a A0b A1a I1a I1b A1b W1 I2a I2b A2 W2 A3 A4a I3b A4b E A5a E E A5b E W3 E I4b E W4 W5 "
-    "E E E E I6b E E W6 A6 W7 A7 E A8 E E A9 E W8 I10b A10 E A11 E E E W9 E E W10 E W11 E E E E E E E E E"
+SCALAR_ORDER = (
+    "I0a T0 T1 I1a T2 T3 T4 T5 I3a I4a I5a I5b T6 T7 X8 I7a I7b T8 T9 X10 X11 I8a T10 T11 I9a I9b I10a I11a I11b"
 )
+VECTOR_ORDER = (
+    "I0b C W0 A0a A0b A1a I1b A1b X2a X2b W1 X3a X3b I2a I2b A2 W2 A3 A4a I3b A5a E E E A4b A5b E W3 E I4b E "
+    "W4 W5 E E E I6a E E I6b E W6 A6 W7 E A7 I8b A8 E E W8 E A9 E A10 A11 E E E W9 I10b E W10 E E W11 "
+    "E E E E E E E E E"
+)
+SORTED_CHUNKS = (2, 3, 8, 10, 11)
+SORT_BUFS = 3
 
 
 def parse(token):
@@ -90,22 +95,24 @@ def vector_order():
             order.append(("empty_c",))
         elif token.startswith("I"):
             order.append(("weave", parse(token)[1], parse(token)[2][0], "vector"))
+        elif token.startswith("X"):
+            order.append(("sort",) + parse(token)[1:] + ("vector",))
         else:
             order.append(("quantise",) + parse(token))
     return order
 
 
 def scalar_order():
-    on_vector = [step[1:3] for step in vector_order() if step[0] == "weave"]
-    halves = [
-        ("weave", chunk, h, "scalar") for chunk in range(CHUNKS) for h in range(2) if (chunk, h) not in on_vector
-    ]
-    order, used = [], 0
-    for pair, count in enumerate(SCALAR_HALVES_BEFORE_PAIR):
-        order += halves[used : used + count]
-        used += count
-        order += [("empty", chunk, h) for chunk in (2 * pair, 2 * pair + 1) for h in range(2)]
-    return order + halves[used:]
+    order = []
+    for token in SCALAR_ORDER.split():
+        letter, chunk, halves = parse(token)
+        if letter == "T":
+            order += [("empty", chunk, h) for h in halves]
+        elif letter == "X":
+            order.append(("sort", chunk, halves, "scalar"))
+        else:
+            order.append(("weave", chunk, halves[0], "scalar"))
+    return order
 
 
 def sync_order():
@@ -124,13 +131,17 @@ def makes(step):
         return [step[:3] + (h,) for h in step[3]]
     if step[0] == "weave":
         return [step[:3]]
+    if step[0] == "sort":
+        return [step[:2] + (h,) for h in step[2]]
     return [step]
 
 
 def needs(step):
     kind = step[0]
     if kind == "turn":
-        return [("load", "A") + step[1:]]
+        return [("sort",) + step[1:] if step[1] in SORTED_CHUNKS else ("load", "A") + step[1:]]
+    if kind == "sort":
+        return [("load", "A", step[1], h) for h in step[2]]
     if kind == "empty":
         return [("turn",) + step[1:]]
     if kind == "empty_c":
@@ -180,6 +191,7 @@ def tile_kronecker_gradient_sketch_s2_kernel(tc, x, g, y, sx, sg, sy, c, r, out)
         keep = ctx.enter_context(tc.tile_pool(name="keep", bufs=1))
         raw_pool = ctx.enter_context(tc.tile_pool(name="raw", bufs=RAW_BUFS))
         stage_pool = ctx.enter_context(tc.tile_pool(name="stage", bufs=STAGE_BUFS))
+        sort_pool = ctx.enter_context(tc.tile_pool(name="sorted", bufs=SORT_BUFS))
         out_pool = ctx.enter_context(tc.tile_pool(name="result", bufs=OUT_BUFS))
         turn_psum = ctx.enter_context(tc.psum_pool(name="turn", bufs=PSUM_BUFS))
         sum_psum = ctx.enter_context(tc.psum_pool(name="sums", bufs=PSUM_BUFS))
@@ -194,6 +206,7 @@ def tile_kronecker_gradient_sketch_s2_kernel(tc, x, g, y, sx, sg, sy, c, r, out)
         c_all = keep.tile([P, R], BF16)
 
         raw, staged, codes, scales, banks, sums, second, results = {}, {}, {}, {}, {}, {}, {}, {}
+        ordered = {}
 
         def source(chunk):
             return sources[chunk // (2 * PASSES)][chunk % PASSES], (chunk // PASSES) % 2
@@ -229,17 +242,35 @@ def tile_kronecker_gradient_sketch_s2_kernel(tc, x, g, y, sx, sg, sy, c, r, out)
                 in_=banks["c"][:].rearrange("p j n -> p n j"),
             )
 
+        def copy_on(engine, dst, src):
+            if engine == "vector":
+                nc.vector.tensor_copy(out=dst, in_=src)
+            else:
+                nc.scalar.copy(out=dst, in_=src)
+
+        def raw_words(chunk):
+            return raw["A", chunk][:].rearrange("p j k -> p (j k)").bitcast(F32)
+
+        def sort(chunk, halves, engine):
+            if halves[0] == 0:
+                ordered[chunk] = sort_pool.tile([P, TILES * 2 * P], F32, name="ordered", align_bytes=256)
+            span = slice(halves[0] * SPAN, (halves[-1] + 1) * SPAN)
+            copy_on(
+                engine,
+                ordered[chunk][:, span].rearrange("p (j u w) -> p j u w", u=2, w=P),
+                raw_words(chunk)[:, span].rearrange("p (j w u) -> p j u w", u=2, w=P),
+            )
+
         def turn(chunk, b):
-            words = raw["A", chunk][:].rearrange("p j k -> p (j k)").bitcast(F32)
             banks[chunk, b] = turn_psum.tile([P, 2, 2 * P], F32, name="bank")
             for t in range(2):
                 first = (2 * b + t) * 2 * P
                 for u in range(2):
-                    nc.tensor.transpose(
-                        banks[chunk, b][:, u, t * P : (t + 1) * P],
-                        words[:, first + u : first + 2 * P : 2],
-                        ident[:],
-                    )
+                    if chunk in SORTED_CHUNKS:
+                        words = ordered[chunk][:, first + u * P : first + (u + 1) * P]
+                    else:
+                        words = raw_words(chunk)[:, first + u : first + 2 * P : 2]
+                    nc.tensor.transpose(banks[chunk, b][:, u, t * P : (t + 1) * P], words, ident[:])
 
         def empty(chunk, b):
             words = stage_tile("A", chunk)[:].bitcast(F32)
@@ -254,10 +285,7 @@ def tile_kronecker_gradient_sketch_s2_kernel(tc, x, g, y, sx, sg, sy, c, r, out)
             src = raw["W", chunk][:, :, h * width : (h + 1) * width]
             dst = dst.rearrange("p (n i t) -> p n t i", i=4, t=PACK)
             src = src.rearrange("p t (n i) -> p n t i", i=4)
-            if engine == "vector":
-                nc.vector.tensor_copy(out=dst, in_=src)
-            else:
-                nc.scalar.copy(out=dst, in_=src)
+            copy_on(engine, dst, src)
 
         def code_format(side, chunk):
             return source(chunk)[0][3] if side == "A" else E4M3X4
@@ -322,7 +350,7 @@ def tile_kronecker_gradient_sketch_s2_kernel(tc, x, g, y, sx, sg, sy, c, r, out)
 
         emit = {
             "load": load, "turn_c": turn_c, "empty_c": empty_c, "turn": turn, "empty": empty, "weave": weave,
-            "quantise": quantise, "mm": mm, "finish": finish, "store": store,
+            "sort": sort, "quantise": quantise, "mm": mm, "finish": finish, "store": store,
         }
         for step in merged([sync_order(), tensor_order(), scalar_order(), vector_order()]):
             emit[step[0]](*step[1:])

@@ -26,18 +26,18 @@ PSUM_BUFS = 4
 STAGE_BUFS = 4
 RAW_BUFS = 8
 OUT_BUFS = 6
-LATE_BY_PASS_QUARTER = 6
+TURN_BANK_QUARTERS = (5, 7)
 
-LOAD_ORDER = "W0 A0a A0b A1a A1b W1 A2 A3 W2 A4 A5 W3 W4 W5 A6 A7 W6 W7 A8 A9 W8 W9 A10 A11 W10 W11"
+LOAD_ORDER = "W0 A0a A0b A1a A1b A2 W1 A3 W2 A4 A5 W3 W4 W5 A6 A7 W6 W7 A8 A9 W8 W9 A10 A11 W10 W11"
 SCALAR_ORDER = (
-    "I0a T0 T1 I1a T2 T3 T4 T5 I3a I4a I5a I5b T6 T7 X8 I7a I7b T8 T9 X10 X11 I8a T10 T11 I9a I9b I10a I11a I11b"
+    "I0a T0 T1 I1a X3b T2 T3 T4 T5 I3a I3b I5a I5b T6 T7 I6a I7a I8a T8 T9 X11 I9a T10 T11 I10a I10b I11a"
 )
 VECTOR_ORDER = (
-    "I0b C W0 A0a A0b A1a I1b A1b X2a X2b W1 X3a X3b I2a I2b A2 W2 A3 A4a I3b A5a E E E A4b A5b E W3 E I4b E "
-    "W4 W5 E E E I6a E E I6b E W6 A6 W7 E A7 I8b A8 E E W8 E A9 E A10 A11 E E E W9 I10b E W10 E E W11 "
-    "E E E E E E E E E"
+    "I0b C W0 A0a A0b X2 A1a I1b A1b X3a W1 I2a I2b A2 A3 W2 A4a A4b A5a E A5b E E E E E I4b W3 W4 W5 E E E E "
+    "I7b X9 W6 A6 W7 A7 E E E E W8 A8 I9b E E W9 A9 A10 A11 E E E E W10 W11 E E E E E E E E E E E E"
 )
-SORTED_CHUNKS = (2, 3, 8, 10, 11)
+GPSIMD_ORDER = (("I4a", "A5b"), ("I6b", "W5"), ("I8b", "A7"), ("I11b", "A11"))
+SORTED_CHUNKS = (2, 3, 9, 11)
 SORT_BUFS = 3
 
 
@@ -60,8 +60,6 @@ def tensor_order():
         return [("mm", quarter, j, k_pass) for j in range(TILES)]
 
     def whole(quarter):
-        if quarter == LATE_BY_PASS_QUARTER:
-            return [step for k_pass in range(PASSES) for step in by_pass(quarter, k_pass)]
         return [("mm", quarter, j, k_pass) for j in range(TILES) for k_pass in range(PASSES)]
 
     after_pair = [
@@ -115,6 +113,14 @@ def scalar_order():
     return order
 
 
+def gpsimd_order():
+    order = []
+    for token, after in GPSIMD_ORDER:
+        order.append(("wait_for",) + parse(after))
+        order.append(("weave", parse(token)[1], parse(token)[2][0], "gpsimd"))
+    return order
+
+
 def sync_order():
     loads = [("load",) + parse(token) for token in LOAD_ORDER.split()]
     stores = [
@@ -148,6 +154,8 @@ def needs(step):
         return [("turn_c",)]
     if kind == "weave":
         return [("load", "W") + step[1:3]]
+    if kind == "wait_for":
+        return [("quantise",) + step[1:3] + (step[3][-1],)]
     if kind == "quantise":
         return [("empty" if step[1] == "A" else "weave", step[2], h) for h in step[3]]
     if kind == "mm":
@@ -204,6 +212,7 @@ def tile_kronecker_gradient_sketch_s2_kernel(tc, x, g, y, sx, sg, sy, c, r, out)
         r_rows = keep.tile([P, 2, TILES], BF16)
         nc.scalar.dma_start(out=r_rows[:], in_=r.rearrange("(h p j) -> p h j", h=2, p=P))
         c_all = keep.tile([P, R], BF16)
+        token = keep.tile([P, 1], U32)
 
         raw, staged, codes, scales, banks, sums, second, results = {}, {}, {}, {}, {}, {}, {}, {}
         ordered = {}
@@ -252,7 +261,7 @@ def tile_kronecker_gradient_sketch_s2_kernel(tc, x, g, y, sx, sg, sy, c, r, out)
             return raw["A", chunk][:].rearrange("p j k -> p (j k)").bitcast(F32)
 
         def sort(chunk, halves, engine):
-            if halves[0] == 0:
+            if chunk not in ordered:
                 ordered[chunk] = sort_pool.tile([P, TILES * 2 * P], F32, name="ordered", align_bytes=256)
             span = slice(halves[0] * SPAN, (halves[-1] + 1) * SPAN)
             copy_on(
@@ -283,9 +292,21 @@ def tile_kronecker_gradient_sketch_s2_kernel(tc, x, g, y, sx, sg, sy, c, r, out)
             width = SPAN // 2
             dst = stage_tile("W", chunk)[:, h * width * PACK : (h + 1) * width * PACK]
             src = raw["W", chunk][:, :, h * width : (h + 1) * width]
-            dst = dst.rearrange("p (n i t) -> p n t i", i=4, t=PACK)
-            src = src.rearrange("p t (n i) -> p n t i", i=4)
-            copy_on(engine, dst, src)
+            if engine == "gpsimd":
+                nc.gpsimd.tensor_scalar(
+                    out=dst.rearrange("p (n t) -> p n t", t=PACK),
+                    in0=src.rearrange("p t n -> p n t"),
+                    scalar1=1.0,
+                    scalar2=0.0,
+                    op0=ALU.mult,
+                    op1=ALU.add,
+                )
+            else:
+                dst = dst.rearrange("p (n i t) -> p n t i", i=4, t=PACK)
+                copy_on(engine, dst, src.rearrange("p t (n i) -> p n t i", i=4))
+
+        def wait_for(side, chunk, halves):
+            nc.gpsimd.tensor_copy(out=token[:], in_=codes[side, chunk][:, SPAN - 1 : SPAN])
 
         def code_format(side, chunk):
             return source(chunk)[0][3] if side == "A" else E4M3X4
@@ -306,7 +327,7 @@ def tile_kronecker_gradient_sketch_s2_kernel(tc, x, g, y, sx, sg, sy, c, r, out)
             factor, m_half, n_half = quarter_parts(quarter)
             a, w = chunk_of(factor, m_half, k_pass), chunk_of(factor, n_half, k_pass)
             if k_pass == 0:
-                pool = turn_psum if quarter == LATE_BY_PASS_QUARTER else sum_psum
+                pool = turn_psum if quarter in TURN_BANK_QUARTERS else sum_psum
                 sums[quarter, j] = pool.tile([P, SPAN], F32, name="bank")
             cols = slice(j * P, (j + 1) * P)
             nc.tensor.matmul_mx(
@@ -350,7 +371,7 @@ def tile_kronecker_gradient_sketch_s2_kernel(tc, x, g, y, sx, sg, sy, c, r, out)
 
         emit = {
             "load": load, "turn_c": turn_c, "empty_c": empty_c, "turn": turn, "empty": empty, "weave": weave,
-            "sort": sort, "quantise": quantise, "mm": mm, "finish": finish, "store": store,
+            "sort": sort, "wait_for": wait_for, "quantise": quantise, "mm": mm, "finish": finish, "store": store,
         }
-        for step in merged([sync_order(), tensor_order(), scalar_order(), vector_order()]):
+        for step in merged([sync_order(), tensor_order(), scalar_order(), vector_order(), gpsimd_order()]):
             emit[step[0]](*step[1:])

from contextlib import ExitStack

import concourse.mybir as mybir
from concourse.masks import make_identity

M, R = 1024, 1024
K_TOTAL = 1024 + 512 + 1536
FLOPS = 2 * M * R * K_TOTAL

F32 = mybir.dt.float32
BF16 = mybir.dt.bfloat16
U32 = mybir.dt.uint32
U8 = mybir.dt.uint8
E4M3X4 = mybir.dt.float8_e4m3fn_x4
E5M2X4 = mybir.dt.float8_e5m2_x4
ALU = mybir.AluOpType

P = 128
PACK = 4
SPAN = P * PACK
PASSES = 3
CHUNKS = 12
TILES = 4
QUARTERS = 8
PSUM_BUFS = 4
STAGE_BUFS = 4
RAW_BUFS = 8
OUT_BUFS = 6
TURN_BANK_QUARTERS = (5, 7)

LOAD_ORDER = "W0 A0a A0b A1a A1b A2 W1 A3 W2 A4 A5 W3 W4 W5 A6 A7 W6 W7 A8 A9 W8 W9 A10 A11 W10 W11"
SCALAR_ORDER = (
    "I0a T0 T1 I1a X3b T2 T3 T4 T5 I3a I3b I5a I5b T6 T7 I6a I7a I8a T8 T9 X11 I9a T10 T11 I10a I10b I11a"
)
VECTOR_ORDER = (
    "I0b C W0 A0a A0b X2 A1a I1b A1b X3a W1 I2a I2b A2 A3 W2 A4a A4b A5a E A5b E E E E E I4b W3 W4 W5 E E E E "
    "I7b X9 W6 A6 W7 A7 E E E E W8 A8 I9b E E W9 A9 A10 A11 E E E E W10 W11 E E E E E E E E E E E E"
)
GPSIMD_ORDER = (("I4a", "A5b"), ("I6b", "W5"), ("I8b", "A7"), ("I11b", "A11"))
SORTED_CHUNKS = (2, 3, 9, 11)
SORT_BUFS = 3


def parse(token):
    if token[-1] in "ab":
        return token[0], int(token[1:-1]), ("ab".index(token[-1]),)
    return token[0], int(token[1:]), (0, 1)


def chunk_of(factor, half, k_pass):
    return (factor * 2 + half) * PASSES + k_pass


def quarter_parts(quarter):
    return quarter // 4, quarter % 2, (quarter // 2) % 2


def tensor_order():
    def by_pass(quarter, k_pass):
        return [("mm", quarter, j, k_pass) for j in range(TILES)]

    def whole(quarter):
        return [("mm", quarter, j, k_pass) for j in range(TILES) for k_pass in range(PASSES)]

    after_pair = [
        by_pass(0, 0),
        by_pass(0, 1),
        by_pass(0, 2) + whole(1),
        whole(2),
        whole(3),
        whole(4) + whole(5) + whole(6) + whole(7),
    ]
    order = [("turn_c",)]
    for pair in range(CHUNKS // 2):
        order += [("turn", chunk, h) for chunk in (2 * pair, 2 * pair + 1) for h in range(2)]
        order += after_pair[pair]
    return order


def column_parts(quarter, j):
    last = quarter == QUARTERS - 1 and j == TILES - 1
    return [(0, SPAN // 2), (SPAN // 2, SPAN)] if last else [(0, SPAN)]


def vector_order():
    order, finished = [], 0
    for token in VECTOR_ORDER.split():
        if token == "E":
            quarter, j = divmod(finished, TILES)
            order += [("finish", quarter, j, part) for part in column_parts(quarter, j)]
            finished += 1
        elif token == "C":
            order.append(("empty_c",))
        elif token.startswith("I"):
            order.append(("weave", parse(token)[1], parse(token)[2][0], "vector"))
        elif token.startswith("X"):
            order.append(("sort",) + parse(token)[1:] + ("vector",))
        else:
            order.append(("quantise",) + parse(token))
    return order


def scalar_order():
    order = []
    for token in SCALAR_ORDER.split():
        letter, chunk, halves = parse(token)
        if letter == "T":
            order += [("empty", chunk, h) for h in halves]
        elif letter == "X":
            order.append(("sort", chunk, halves, "scalar"))
        else:
            order.append(("weave", chunk, halves[0], "scalar"))
    return order


def gpsimd_order():
    order = []
    for token, after in GPSIMD_ORDER:
        order.append(("wait_for",) + parse(after))
        order.append(("weave", parse(token)[1], parse(token)[2][0], "gpsimd"))
    return order


def sync_order():
    loads = [("load",) + parse(token) for token in LOAD_ORDER.split()]
    stores = [
        ("store", quarter, j, part)
        for quarter in range(QUARTERS // 2, QUARTERS)
        for j in range(TILES)
        for part in column_parts(quarter, j)
    ]
    return loads + stores


def makes(step):
    if step[0] in ("load", "quantise"):
        return [step[:3] + (h,) for h in step[3]]
    if step[0] == "weave":
        return [step[:3]]
    if step[0] == "sort":
        return [step[:2] + (h,) for h in step[2]]
    return [step]


def needs(step):
    kind = step[0]
    if kind == "turn":
        return [("sort",) + step[1:] if step[1] in SORTED_CHUNKS else ("load", "A") + step[1:]]
    if kind == "sort":
        return [("load", "A", step[1], h) for h in step[2]]
    if kind == "empty":
        return [("turn",) + step[1:]]
    if kind == "empty_c":
        return [("turn_c",)]
    if kind == "weave":
        return [("load", "W") + step[1:3]]
    if kind == "wait_for":
        return [("quantise",) + step[1:3] + (step[3][-1],)]
    if kind == "quantise":
        return [("empty" if step[1] == "A" else "weave", step[2], h) for h in step[3]]
    if kind == "mm":
        factor, m_half, n_half = quarter_parts(step[1])
        weights = chunk_of(factor, n_half, step[3])
        return [
            ("quantise", "A", chunk_of(factor, m_half, step[3]), step[2] // 2),
            ("quantise", "W", weights, 0),
            ("quantise", "W", weights, 1),
        ]
    if kind == "finish":
        return [("mm", step[1], step[2], PASSES - 1)]
    if kind == "store":
        return [("finish",) + step[1:]]
    return []


def merged(orders):
    made, text = set(), []
    position = [0] * len(orders)
    while len(text) < sum(len(order) for order in orders):
        before = len(text)
        for e, order in enumerate(orders):
            if position[e] < len(order) and all(key in made for key in needs(order[position[e]])):
                text.append(order[position[e]])
                position[e] += 1
                for key in makes(text[-1]):
                    made.add(key)
        assert len(text) > before
    return text


def tile_kronecker_gradient_sketch_s2_kernel(tc, x, g, y, sx, sg, sy, c, r, out):
    nc = tc.nc
    sources = [
        [(y, sy, 0, E4M3X4), (y, sy, SPAN, E4M3X4), (y, sy, 2 * SPAN, E4M3X4)],
        [(x, sx, 0, E4M3X4), (x, sx, SPAN, E4M3X4), (g, sg, 0, E5M2X4)],
    ]

    with ExitStack() as ctx:
        keep = ctx.enter_context(tc.tile_pool(name="keep", bufs=1))
        raw_pool = ctx.enter_context(tc.tile_pool(name="raw", bufs=RAW_BUFS))
        stage_pool = ctx.enter_context(tc.tile_pool(name="stage", bufs=STAGE_BUFS))
        sort_pool = ctx.enter_context(tc.tile_pool(name="sorted", bufs=SORT_BUFS))
        out_pool = ctx.enter_context(tc.tile_pool(name="result", bufs=OUT_BUFS))
        turn_psum = ctx.enter_context(tc.psum_pool(name="turn", bufs=PSUM_BUFS))
        sum_psum = ctx.enter_context(tc.psum_pool(name="sums", bufs=PSUM_BUFS))
        ctx.enter_context(tc.manual_schedule())

        ident = keep.tile([P, P], F32)
        make_identity(nc, ident[:])
        c_rows = keep.tile([P, R // P], BF16)
        nc.scalar.dma_start(out=c_rows[:], in_=c.rearrange("(p j) -> p j", p=P))
        r_rows = keep.tile([P, 2, TILES], BF16)
        nc.scalar.dma_start(out=r_rows[:], in_=r.rearrange("(h p j) -> p h j", h=2, p=P))
        c_all = keep.tile([P, R], BF16)
        token = keep.tile([P, 1], U32)

        raw, staged, codes, scales, banks, sums, second, results = {}, {}, {}, {}, {}, {}, {}, {}
        ordered = {}

        def source(chunk):
            return sources[chunk // (2 * PASSES)][chunk % PASSES], (chunk // PASSES) % 2

        def stage_tile(side, chunk):
            if (side, chunk) not in staged:
                staged[side, chunk] = stage_pool.tile(
                    [P, SPAN * PACK], BF16, name="staged_" + side, align_bytes=256
                )
            return staged[side, chunk]

        def load(side, chunk, halves):
            (samples, weights, k0, fmt), half = source(chunk)
            span = slice(half * SPAN, (half + 1) * SPAN)
            k_span = slice(k0, k0 + SPAN)
            rows = samples[span, k_span] if side == "A" else weights[k_span, span]
            if halves[0] == 0:
                raw[side, chunk] = raw_pool.tile([P, PACK, SPAN], BF16, name="raw_" + side, align_bytes=256)
            js = slice(2 * halves[0], 2 * halves[-1] + 2)
            nc.sync.dma_start(
                out=raw[side, chunk][:, js, :], in_=rows.rearrange("(p j) w -> p j w", j=PACK)[:, js, :]
            )

        def turn_c():
            words = c_rows[:].bitcast(F32)
            banks["c"] = turn_psum.tile([P, 4, P], F32, name="bank")
            for j in range(4):
                nc.tensor.transpose(banks["c"][:, j, :], words[:, j : j + 1].to_broadcast([P, P]), ident[:])

        def empty_c():
            nc.vector.tensor_copy(
                out=c_all[:].bitcast(F32).rearrange("p (n j) -> p n j", j=4),
                in_=banks["c"][:].rearrange("p j n -> p n j"),
            )

        def copy_on(engine, dst, src):
            if engine == "vector":
                nc.vector.tensor_copy(out=dst, in_=src)
            else:
                nc.scalar.copy(out=dst, in_=src)

        def raw_words(chunk):
            return raw["A", chunk][:].rearrange("p j k -> p (j k)").bitcast(F32)

        def sort(chunk, halves, engine):
            if chunk not in ordered:
                ordered[chunk] = sort_pool.tile([P, TILES * 2 * P], F32, name="ordered", align_bytes=256)
            span = slice(halves[0] * SPAN, (halves[-1] + 1) * SPAN)
            copy_on(
                engine,
                ordered[chunk][:, span].rearrange("p (j u w) -> p j u w", u=2, w=P),
                raw_words(chunk)[:, span].rearrange("p (j w u) -> p j u w", u=2, w=P),
            )

        def turn(chunk, b):
            banks[chunk, b] = turn_psum.tile([P, 2, 2 * P], F32, name="bank")
            for t in range(2):
                first = (2 * b + t) * 2 * P
                for u in range(2):
                    if chunk in SORTED_CHUNKS:
                        words = ordered[chunk][:, first + u * P : first + (u + 1) * P]
                    else:
                        words = raw_words(chunk)[:, first + u : first + 2 * P : 2]
                    nc.tensor.transpose(banks[chunk, b][:, u, t * P : (t + 1) * P], words, ident[:])

        def empty(chunk, b):
            words = stage_tile("A", chunk)[:].bitcast(F32)
            nc.scalar.copy(
                out=words[:, b * SPAN : (b + 1) * SPAN].rearrange("p (m u) -> p m u", u=2),
                in_=banks[chunk, b][:].rearrange("p u m -> p m u"),
            )

        def weave(chunk, h, engine):
            width = SPAN // 2
            dst = stage_tile("W", chunk)[:, h * width * PACK : (h + 1) * width * PACK]
            src = raw["W", chunk][:, :, h * width : (h + 1) * width]
            if engine == "gpsimd":
                nc.gpsimd.tensor_scalar(
                    out=dst.rearrange("p (n t) -> p n t", t=PACK),
                    in0=src.rearrange("p t n -> p n t"),
                    scalar1=1.0,
                    scalar2=0.0,
                    op0=ALU.mult,
                    op1=ALU.add,
                )
            else:
                dst = dst.rearrange("p (n i t) -> p n t i", i=4, t=PACK)
                copy_on(engine, dst, src.rearrange("p t (n i) -> p n t i", i=4))

        def wait_for(side, chunk, halves):
            nc.gpsimd.tensor_copy(out=token[:], in_=codes[side, chunk][:, SPAN - 1 : SPAN])

        def code_format(side, chunk):
            return source(chunk)[0][3] if side == "A" else E4M3X4

        def quantise(side, chunk, halves):
            if halves[0] == 0:
                label = "%s%d" % (side, chunk)
                codes[side, chunk] = keep.tile([P, SPAN], U32, name="codes_" + label, align_bytes=256)
                scales[side, chunk] = keep.tile([P, SPAN], U8, name="scales_" + label, align_bytes=256)
            first, end = halves[0] * SPAN // 2, (halves[-1] + 1) * SPAN // 2
            nc.vector.quantize_mx(
                out=codes[side, chunk][:, first:end].bitcast(code_format(side, chunk)),
                scales=scales[side, chunk][:, first:end],
                in_=staged[side, chunk][:, first * PACK : end * PACK],
            )

        def mm(quarter, j, k_pass):
            factor, m_half, n_half = quarter_parts(quarter)
            a, w = chunk_of(factor, m_half, k_pass), chunk_of(factor, n_half, k_pass)
            if k_pass == 0:
                pool = turn_psum if quarter in TURN_BANK_QUARTERS else sum_psum
                sums[quarter, j] = pool.tile([P, SPAN], F32, name="bank")
            cols = slice(j * P, (j + 1) * P)
            nc.tensor.matmul_mx(
                out=sums[quarter, j][:],
                lhsT=codes["A", a][:, cols].bitcast(code_format("A", a)),
                lhsT_scale=scales["A", a][:, cols],
                rhs=codes["W", w][:].bitcast(E4M3X4),
                rhs_scale=scales["W", w][:],
                start=(k_pass == 0),
                stop=(k_pass == PASSES - 1),
            )

        def finish(quarter, j, part):
            factor, m_half, n_half = quarter_parts(quarter)
            if factor == 0:
                second[quarter, j] = keep.tile([P, SPAN], F32, name="second_%d_%d" % (quarter, j))
                nc.vector.tensor_tensor(
                    out=second[quarter, j][:],
                    in0=sums[quarter, j][:],
                    in1=c_all[:, n_half * SPAN : (n_half + 1) * SPAN],
                    op=ALU.add,
                )
            else:
                cols = slice(*part)
                results[quarter, j, part] = out_pool.tile([P, part[1] - part[0]], F32, name="result")
                nc.vector.scalar_tensor_tensor(
                    out=results[quarter, j, part][:],
                    in0=sums[quarter, j][:, cols],
                    scalar=r_rows[:, m_half, j : j + 1],
                    in1=second[quarter - QUARTERS // 2, j][:, cols],
                    op0=ALU.mult,
                    op1=ALU.mult,
                )

        def store(quarter, j, part):
            factor, m_half, n_half = quarter_parts(quarter)
            block = out[m_half * SPAN : (m_half + 1) * SPAN, n_half * SPAN + part[0] : n_half * SPAN + part[1]]
            nc.sync.dma_start(
                out=block.rearrange("(p j) n -> p j n", j=TILES)[:, j, :], in_=results[quarter, j, part][:]
            )

        emit = {
            "load": load, "turn_c": turn_c, "empty_c": empty_c, "turn": turn, "empty": empty, "weave": weave,
            "sort": sort, "wait_for": wait_for, "quantise": quantise, "mm": mm, "finish": finish, "store": store,
        }
        for step in merged([sync_order(), tensor_order(), scalar_order(), vector_order(), gpsimd_order()]):
            emit[step[0]](*step[1:])
